import numpy as np
import ml_dtypes


def mxq(x, axis, fmt="e4m3"):
    dtype, down = {"e4m3": (ml_dtypes.float8_e4m3fn, 7), "e5m2": (ml_dtypes.float8_e5m2, 14)}[fmt]
    v = np.moveaxis(np.asarray(x, np.float32).astype(ml_dtypes.bfloat16).astype(np.float64), axis, -1)
    blocks = v.reshape(v.shape[:-1] + (-1, 32))
    amax = np.abs(blocks).max(-1, keepdims=True)
    byte = np.maximum(np.where(amax > 0, np.frexp(amax)[1] - 1 + 127, 0) - down, 1)
    scale = np.exp2(byte - 127.0)
    codes = (blocks / scale).astype(np.float32).astype(dtype).astype(np.float64)
    return np.moveaxis((codes * scale).reshape(v.shape), -1, axis)


WIDE = False


def mx_kscale(k):
    if not WIDE:
        return np.ones(k)
    levels = np.array([10, -10, 5, -5, 0])
    if k % 512:
        return np.exp2(np.random.permutation(np.resize(levels, k // 32))).repeat(32)
    a = np.empty((k // 512, 16))
    for p in range(k // 512):
        a[p, :8] = np.random.permutation(np.resize(levels, 8))
        for g in range(8):
            far = levels[np.abs(levels - a[p, g]) >= 10]
            a[p, g + 8] = far[np.random.randint(len(far))]
    return np.exp2(a.ravel()).repeat(32)


def f64(x):
    return np.asarray(x).astype(np.float64)


def striped(idx):
    return np.tile(idx.reshape(-1, 16).T, (8, 1)).astype(np.uint16)


def unstriped(offs):
    return offs[:16].T.reshape(-1).astype(np.int64)


E2M1 = np.array([0.0, 0.5, 1.0, 1.5, 2.0, 3.0, 4.0, 6.0, -0.0, -0.5, -1.0, -1.5, -2.0, -3.0, -4.0, -6.0])


def pack_weight(w, fmt):
    k, n = w.shape
    w = f64(np.asarray(w, np.float32).astype(ml_dtypes.bfloat16)).reshape(k // 32, 32, n)
    amax = np.abs(w).max(1)
    if fmt == "e4m3":
        byte = np.frexp(amax)[1] - 1 + 127 - 7
    else:
        mant, ex = np.frexp(amax / 6.0)
        byte = np.where(mant > 0.5, ex, ex - 1) + 127
    byte = np.clip(np.where(amax > 0, byte, 1), 1, 254)
    scaled = (w * np.exp2(127.0 - byte)[:, None, :]).reshape(k, n).astype(np.float32)
    by_word = np.ascontiguousarray(scaled.reshape(k // 512, 128, 4, n).transpose(0, 1, 3, 2))
    if fmt == "e4m3":
        words = by_word.astype(ml_dtypes.float8_e4m3fn).view(np.uint8)
    else:
        c = by_word.astype(ml_dtypes.float4_e2m1fn).view(np.uint8) & 0xF
        words = (c[..., 0::2] | (c[..., 1::2] << 4)).reshape(k // 512, 128, 2 * n)
    return np.ascontiguousarray(words), np.ascontiguousarray(byte.astype(np.uint8).reshape(k // 512, 16, n))


def unpack_weight(words, scales, fmt):
    g, _, n = scales.shape
    words = np.ascontiguousarray(words).reshape(g, 128, n, -1)
    if fmt == "e4m3":
        vals = words.view(ml_dtypes.float8_e4m3fn).astype(np.float64)
    else:
        nib = np.empty((g, 128, n, 4), np.uint8)
        nib[..., 0::2] = words & 0xF
        nib[..., 1::2] = words >> 4
        vals = E2M1[nib]
    vals = vals * np.repeat(np.exp2(scales.astype(np.float64) - 127.0), 8, axis=1)[..., None]
    return vals.transpose(0, 1, 3, 2).reshape(g * 512, n)


K, T, E, C = 512, 768, 6, 256


def deal():
    first = np.random.permutation(np.repeat(np.arange(E), T // E))
    second = (first + 1 + np.random.permutation(np.repeat(np.arange(E - 1), -(-T // (E - 1)))[:T])) % E
    while np.bincount(second, minlength=E).max() != T // E:
        load = np.bincount(second, minlength=E); hi, lo = int(load.argmax()), int(load.argmin())
        t = np.flatnonzero((second == hi) & (first != lo))[0]; second[t] = lo
    slot_token = np.empty(E * C, np.int64); pos = np.empty((2, T), np.int64); fill = np.zeros(E, np.int64)
    place = np.stack([np.random.permutation(C) for _ in range(E)])
    for r, deal in enumerate((first, second)):
        for t in np.random.permutation(T):
            e = deal[t]; j = e * C + place[e, fill[e]]; fill[e] += 1; slot_token[j] = t; pos[r, t] = j
    g = np.random.uniform(0.2, 0.8, T)
    return slot_token, pos, np.stack([g, 1.0 - g])


def by_expert(wq, xq):
    return np.concatenate([wq[e].T @ xq[:, e * C:(e + 1) * C] for e in range(E)], axis=1)


def setup_inputs():
    n = np.random.standard_normal
    s = mx_kscale(K)
    slots1, pos1, g1 = deal()
    slots2, pos2, g2 = deal()
    x = pack_weight(n((K, T)) * s[:, None], "e4m3")
    w = [pack_weight(m, "e4m3") for m in n((E, K, K)) / np.sqrt(K) / s[None, :, None] * s]
    return {
        "x_words": x[0],
        "x_scales": x[1],
        "w_words": np.stack([m[0] for m in w]),
        "w_scales": np.stack([m[1] for m in w]),
        "gate1": (np.stack([np.tile(r, (128, 1)) for r in g1])).astype(np.float32),
        "gate2": (np.stack([np.tile(r, (128, 1)) for r in g2])).astype(np.float32),
        "offs": striped(slots1),
        "pos1": striped(pos1[0]),
        "pos2": striped(pos1[1]),
        "offs2": striped(slots2),
        "pos3": striped(pos2[0]),
        "pos4": striped(pos2[1]),
    }


def reference(x_words, x_scales, w_words, w_scales, gate1, gate2, offs, pos1, pos2, offs2, pos3, pos4):
    w = np.stack([unpack_weight(w_words[e], w_scales[e], "e4m3") for e in range(E)])
    idx, idx2 = unstriped(offs), unstriped(offs2)
    y = by_expert(w, unpack_weight(x_words, x_scales, "e4m3")[:, idx])
    c = sum(f64(gate1[r, :1]) * y[:, unstriped(p)] for r, p in enumerate((pos1, pos2)))
    z = by_expert(w, mxq(c[:, idx2], 0, "e4m3"))
    out = sum(f64(gate2[r, :1]) * z[:, unstriped(p)] for r, p in enumerate((pos3, pos4)))
    return out

@@ -1,0 +1,277 @@
+from contextlib import ExitStack
+
+import concourse.mybir as mybir
+from concourse.masks import make_identity
+
+K, T, E, C = 512, 768, 6, 256
+S = E * C
+FLOPS = 2 * 2 * K * K * S
+
+F32 = mybir.dt.float32
+BF16 = mybir.dt.bfloat16
+I32 = mybir.dt.int32
+U32 = mybir.dt.uint32
+U16 = mybir.dt.uint16
+U8 = mybir.dt.uint8
+FP8X4 = mybir.dt.float8_e4m3fn_x4
+MULT = mybir.AluOpType.mult
+ADD = mybir.AluOpType.add
+COPY = mybir.ActivationFunctionType.Copy
+
+P = 128
+PACK = 4
+BANK = 512
+HALF = T // 2
+
+
+def entries(tile, a, b):
+    return tile[:, a // 16 : b // 16]
+
+
+def tile_moe_uni_none_kernel(
+    tc, x_words, x_scales, w_words, w_scales, gate1, gate2, offs, pos1, pos2, offs2, pos3, pos4, out
+):
+    nc = tc.nc
+    with ExitStack() as ctx:
+        lists = ctx.enter_context(tc.tile_pool(name="lists", bufs=1))
+        keep = ctx.enter_context(tc.tile_pool(name="keep", bufs=1))
+        work = ctx.enter_context(tc.tile_pool(name="work", bufs=2))
+        psum = ctx.enter_context(tc.psum_pool(name="psum", bufs=1))
+
+        banks = [psum.tile([P, BANK], F32, name=f"bank{b}") for b in range(8)]
+
+        def load_list(src, name):
+            tile = lists.tile([P, src.shape[1]], U16, name=name)
+            nc.sync.dma_start(tile[:], src)
+            return tile
+
+        xs = keep.tile([P, T // 4], I32, name="xs", align_bytes=64)
+        ws = [keep.tile([P, K // 4], I32, name=f"ws{b}", align_bytes=64) for b in range(2)]
+        nc.gpsimd.memset(xs[:], 0)
+        nc.gpsimd.memset(ws[0][:], 0)
+        nc.gpsimd.memset(ws[1][:], 0)
+
+        ident = keep.tile([P, P], F32, name="ident")
+        make_identity(nc, ident[:])
+
+        offs_t = load_list(offs, "offs_t")
+        xw = keep.tile([P, T], I32, name="xw", align_bytes=64)
+        nc.sync.dma_start(xw[:], x_words[0].rearrange("p t d -> p (t d)").bitcast(I32))
+        xs_rows = x_scales[0].bitcast(I32)
+        for q in range(4):
+            nc.sync.dma_start(xs[32 * q : 32 * q + 4, :], xs_rows[4 * q : 4 * q + 4, :])
+
+        w_raw = [keep.tile([P, 2, K], I32, name=f"w_raw{g}", align_bytes=64) for g in range(3)]
+
+        def load_words(g):
+            nc.sync.dma_start(
+                w_raw[g][:], w_words[2 * g : 2 * g + 2, 0].rearrange("e p i d -> p e (i d)").bitcast(I32)
+            )
+
+        def load_scales(b):
+            n = min(4, E - 4 * b)
+            for q in range(4):
+                nc.sync.dma_start(
+                    ws[b][32 * q : 32 * q + 4 * n, :],
+                    w_scales[4 * b : 4 * b + n, 0, 4 * q : 4 * q + 4, :].bitcast(I32),
+                )
+
+        load_words(0)
+        load_scales(0)
+        load_words(1)
+        load_words(2)
+        load_scales(1)
+
+        pos1_t = load_list(pos1, "pos1_t")
+        g1 = [keep.tile([P, T], F32, name=f"g1_{r}") for r in range(2)]
+        nc.sync.dma_start(g1[0][:], gate1[0])
+        pos2_t = load_list(pos2, "pos2_t")
+        nc.sync.dma_start(g1[1][:], gate1[1])
+        offs2_t = load_list(offs2, "offs2_t")
+        pos3_t = load_list(pos3, "pos3_t")
+        pos4_t = load_list(pos4, "pos4_t")
+        g2 = [keep.tile([P, T], F32, name=f"g2_{r}") for r in range(2)]
+        nc.sync.dma_start(g2[0][:], gate2[0])
+        nc.sync.dma_start(g2[1][:], gate2[1])
+
+        gw = [keep.tile([P, 2 * C], U32, name=f"gw{g}", align_bytes=64) for g in range(3)]
+        gs = [keep.tile([P, 2 * C], U8, name=f"gs{g}", align_bytes=64) for g in range(3)]
+        wp = [keep.tile([P, 2, PACK, P], I32, name=f"wp{g}", align_bytes=64) for g in range(2)]
+        wp_first = keep.tile([P, 2, P], I32, name="wp_first", align_bytes=64)
+        wp_rest = keep.tile([P, 2, PACK - 1, P], I32, name="wp_rest", align_bytes=64)
+        sp = [keep.tile([P, PACK, P], U8, name=f"sp{b}", align_bytes=64) for b in range(2)]
+
+        def gather_words(g):
+            a = 2 * C * g
+            nc.vector.tensor_copy(gw[g][:], xw[:].bitcast(U32).indirect(entries(offs_t, a, a + 2 * C)))
+
+        def gather_bytes(g, a, b):
+            base = 2 * C * g
+            nc.vector.tensor_copy(
+                gs[g][:, a:b], xs[:].bitcast(U8).indirect(entries(offs_t, base + a, base + b))
+            )
+
+        def permute_words(g):
+            nc.vector.tensor_copy(
+                wp[g][:].rearrange("p e t m -> p e m t"),
+                w_raw[g][:].rearrange("p e (m t) -> p e m t", t=PACK),
+            )
+
+        def permute_scales(b):
+            nc.vector.tensor_copy(sp[b][:], ws[b][:].bitcast(U8).rearrange("p (m t) -> p t m", t=PACK))
+
+        def weight(e, t):
+            if e < 4:
+                codes = wp[e // 2][:, e % 2, t, :]
+            elif t == 0:
+                codes = wp_first[:, e % 2, :]
+            else:
+                codes = wp_rest[:, e % 2, t - 1, :]
+            return codes.bitcast(FP8X4), sp[e // 4][4 * (e % 4) :, t, :]
+
+        def product(dst, t, bank, a, b, codes, scales):
+            col = 0
+            s = a
+            while s < b:
+                e = s // C
+                n = min(b, (e + 1) * C) - s
+                lhs, lhs_scale = weight(e, t)
+                rhs, rhs_scale = codes(s, s + n), scales(s, s + n)
+                nc.tensor.matmul_mx(
+                    out=banks[bank][:, col : col + n],
+                    lhsT=lhs,
+                    lhsT_scale=lhs_scale,
+                    rhs=rhs.bitcast(FP8X4),
+                    rhs_scale=rhs_scale,
+                    start=True,
+                    stop=True,
+                )
+                col += n
+                s += n
+            nc.scalar.copy(dst[t][:, a:b], banks[bank][:, 0 : b - a])
+
+        y = [keep.tile([P, S], F32, name=f"y{t}") for t in range(PACK)]
+
+        def x_codes(a, b):
+            return gw[a // (2 * C)][:, a % (2 * C) : a % (2 * C) + b - a]
+
+        def x_scale(a, b):
+            return gs[a // (2 * C)][:, a % (2 * C) : a % (2 * C) + b - a]
+
+        gather_words(0)
+        gather_words(1)
+        permute_words(0)
+        permute_scales(0)
+        gather_bytes(0, 0, 512)
+        product(y, 0, 0, 0, 512, x_codes, x_scale)
+        gather_words(2)
+        permute_words(1)
+        gather_bytes(1, 0, 512)
+        product(y, 0, 4, 512, 1024, x_codes, x_scale)
+        w_last = w_raw[2][:].rearrange("p e (m t) -> p e m t", t=PACK)
+        nc.vector.tensor_copy(wp_first[:], w_last[:, :, :, 0])
+        permute_scales(1)
+        gather_bytes(2, 0, 256)
+        product(y, 0, 5, 1024, 1280, x_codes, x_scale)
+        gather_bytes(2, 256, 384)
+        product(y, 0, 6, 1280, 1408, x_codes, x_scale)
+        gather_bytes(2, 384, 512)
+        product(y, 0, 7, 1408, 1536, x_codes, x_scale)
+        nc.vector.tensor_copy(wp_rest[:].rearrange("p e t m -> p e m t"), w_last[:, :, :, 1:PACK])
+        for t in range(1, PACK):
+            product(y, t, t, 0, 512, x_codes, x_scale)
+            product(y, t, 6, 512, 1024, x_codes, x_scale)
+            product(y, t, 7, 1024, 1536, x_codes, x_scale)
+
+        def weighted(dst, src, pos, gate, a, b):
+            nc.vector.tensor_tensor(dst[:, a:b], src[:].indirect(entries(pos, a, b)), gate[:, a:b], MULT)
+
+        c = [keep.tile([P, T], BF16, name=f"c{t}", align_bytes=64) for t in range(PACK)]
+        pairs = [keep.tile([P, 2, C, 2], BF16, name=f"pairs{e}", align_bytes=64) for e in range(E)]
+        quads = [keep.tile([P, C, PACK], BF16, name=f"quads{e}", align_bytes=64) for e in range(E)]
+        cw = [keep.tile([P, C], U32, name=f"cw{e}", align_bytes=64) for e in range(E)]
+        cs = [keep.tile([P, C], U8, name=f"cs{e}", align_bytes=64) for e in range(E)]
+        z = [keep.tile([P, S], F32, name=f"z{t}") for t in range(PACK)]
+
+        def c_codes(a, b):
+            return cw[a // C][:, a % C : a % C + b - a]
+
+        def c_scale(a, b):
+            return cs[a // C][:, a % C : a % C + b - a]
+
+        def gather_plane(t, e, a, b):
+            nc.scalar.activation(
+                pairs[e][:, t // 2, a:b, t % 2], c[t][:].indirect(entries(offs2_t, e * C + a, e * C + b)), COPY
+            )
+
+        def quantise(e, a, b):
+            nc.vector.tensor_copy(
+                quads[e][:, a:b, :].rearrange("p s (u j) -> p s u j", u=2),
+                pairs[e][:, :, a:b, :].rearrange("p u s j -> p s u j"),
+            )
+            nc.vector.quantize_mx(
+                out=cw[e][:, a:b].bitcast(FP8X4),
+                scales=cs[e][:, a:b],
+                in_=quads[e][:, a:b, :].rearrange("p s j -> p (s j)"),
+            )
+
+        for t in range(PACK):
+            pa = work.tile([P, T], F32, name="pa")
+            pb = work.tile([P, T], F32, name="pb")
+            weighted(pa, y[t], pos1_t, g1[0], 0, 128)
+            weighted(pa, y[t], pos1_t, g1[0], 128, T)
+            if t < PACK - 1:
+                weighted(pb, y[t], pos2_t, g1[1], 0, T)
+                nc.vector.tensor_tensor(c[t][:], pa[:], pb[:], ADD)
+                for e in range(E):
+                    gather_plane(t, e, 0, C)
+            else:
+                weighted(pb, y[t], pos2_t, g1[1], 0, 640)
+                weighted(pb, y[t], pos2_t, g1[1], 640, T)
+                nc.vector.tensor_tensor(c[t][:, 0:512], pa[:, 0:512], pb[:, 0:512], ADD)
+                nc.vector.tensor_tensor(c[t][:, 512:T], pa[:, 512:T], pb[:, 512:T], ADD)
+
+        pieces = [(e, 0, C) for e in range(E - 1)] + [(E - 1, 0, 128), (E - 1, 128, C)]
+        for e, a, b in pieces:
+            gather_plane(PACK - 1, e, a, b)
+        for e, a, b in pieces:
+            quantise(e, a, b)
+        product(z, 0, 0, 0, 512, c_codes, c_scale)
+        product(z, 0, 1, 512, 1024, c_codes, c_scale)
+        product(z, 0, 2, 1024, 1280, c_codes, c_scale)
+        product(z, 0, 3, 1280, 1408, c_codes, c_scale)
+        product(z, 0, 4, 1408, 1536, c_codes, c_scale)
+        for t in range(1, PACK):
+            for g in range(3):
+                product(z, t, 3 + g, 512 * g, 512 * (g + 1), c_codes, c_scale)
+
+        out_rows = out.rearrange("(p t) n -> t p n", t=PACK)
+        for t in range(PACK):
+            pa = work.tile([P, T], F32, name="pa")
+            pb = work.tile([P, T], F32, name="pb")
+            res = keep.tile([P, T], F32, name=f"res{t}")
+            if t < PACK - 1:
+                turned = work.tile([P, T], F32, name="turned")
+                for h in range(2):
+                    a, b = h * HALF, (h + 1) * HALF
+                    weighted(pa, z[t], pos3_t, g2[0], a, b)
+                    weighted(pb, z[t], pos4_t, g2[1], a, b)
+                    for j in range(a, b, P):
+                        dst = banks[h][:, j - a : j - a + P]
+                        nc.tensor.matmul(dst, pa[:, j : j + P], ident[:], start=True, stop=False, is_transpose=True)
+                        nc.tensor.matmul(dst, pb[:, j : j + P], ident[:], start=False, stop=True, is_transpose=True)
+                    nc.scalar.copy(turned[:, a:b], banks[h][:, 0:HALF])
+                    for j in range(a, b, P):
+                        nc.tensor.transpose(banks[6 + h][:, j - a : j - a + P], turned[:, j : j + P], ident[:])
+                    nc.scalar.copy(res[:, a:b], banks[6 + h][:, 0:HALF])
+                    nc.sync.dma_start(out_rows[t][:, a:b], res[:, a:b])
+            else:
+                weighted(pa, z[t], pos3_t, g2[0], 0, 128)
+                weighted(pa, z[t], pos3_t, g2[0], 128, 512)
+                weighted(pb, z[t], pos4_t, g2[1], 0, 512)
+                weighted(pa, z[t], pos3_t, g2[0], 512, T)
+                nc.vector.tensor_tensor(res[:, 0:512], pa[:, 0:512], pb[:, 0:512], ADD)
+                nc.sync.dma_start(out_rows[t][:, 0:512], res[:, 0:512])
+                weighted(pb, z[t], pos4_t, g2[1], 512, T)
+                nc.vector.tensor_tensor(res[:, 512:T], pa[:, 512:T], pb[:, 512:T], ADD)
+                nc.sync.dma_start(out_rows[t][:, 512:T], res[:, 512:T])

@@ -22,6 +22,8 @@ P = 128
 PACK = 4
 BANK = 512
 HALF = T // 2
+RAW = 2 * K * 4
+TAIL = ((0, 384), (384, 640), (640, T))
 
 
 def entries(tile, a, b):
@@ -36,6 +38,7 @@ def tile_moe_uni_none_kernel(
         lists = ctx.enter_context(tc.tile_pool(name="lists", bufs=1))
         keep = ctx.enter_context(tc.tile_pool(name="keep", bufs=1))
         work = ctx.enter_context(tc.tile_pool(name="work", bufs=2))
+        shared = ctx.enter_context(tc.tile_pool(name="shared", bufs=1))
         psum = ctx.enter_context(tc.psum_pool(name="psum", bufs=1))
 
         banks = [psum.tile([P, BANK], F32, name=f"bank{b}") for b in range(8)]
@@ -47,21 +50,13 @@ def tile_moe_uni_none_kernel(
 
         xs = keep.tile([P, T // 4], I32, name="xs", align_bytes=64)
         ws = [keep.tile([P, K // 4], I32, name=f"ws{b}", align_bytes=64) for b in range(2)]
-        nc.gpsimd.memset(xs[:], 0)
-        nc.gpsimd.memset(ws[0][:], 0)
-        nc.gpsimd.memset(ws[1][:], 0)
-
-        ident = keep.tile([P, P], F32, name="ident")
-        make_identity(nc, ident[:])
+        nc.vector.memset(ws[0][:], 0)
+        nc.vector.memset(ws[1][:], 0)
 
         offs_t = load_list(offs, "offs_t")
         xw = keep.tile([P, T], I32, name="xw", align_bytes=64)
         nc.sync.dma_start(xw[:], x_words[0].rearrange("p t d -> p (t d)").bitcast(I32))
-        xs_rows = x_scales[0].bitcast(I32)
-        for q in range(4):
-            nc.sync.dma_start(xs[32 * q : 32 * q + 4, :], xs_rows[4 * q : 4 * q + 4, :])
-
-        w_raw = [keep.tile([P, 2, K], I32, name=f"w_raw{g}", align_bytes=64) for g in range(3)]
+        w_raw = [shared.tile([P, 2, K], I32, name=f"w_raw{g}", align_bytes=64, offset=RAW * g) for g in range(3)]
 
         def load_words(g):
             nc.sync.dma_start(
@@ -71,35 +66,49 @@ def tile_moe_uni_none_kernel(
         def load_scales(b):
             n = min(4, E - 4 * b)
             for q in range(4):
-                nc.sync.dma_start(
+                nc.scalar.dma_start(
                     ws[b][32 * q : 32 * q + 4 * n, :],
                     w_scales[4 * b : 4 * b + n, 0, 4 * q : 4 * q + 4, :].bitcast(I32),
                 )
 
+        xs_rows = x_scales[0].bitcast(I32)
+
+        def load_token_scales(q, queue):
+            queue.dma_start(
+                xs[32 * q : 32 * q + 32, :], xs_rows[4 * q : 4 * q + 4, :].unsqueeze(0).to_broadcast([8, 4, T // 4])
+            )
+
+        ident = keep.tile([P, P], F32, name="ident")
+        make_identity(nc, ident[:])
+
         load_words(0)
         load_scales(0)
+        for q in range(4):
+            load_token_scales(q, nc.sync if q < 2 else nc.scalar)
         load_words(1)
         load_words(2)
         load_scales(1)
 
-        pos1_t = load_list(pos1, "pos1_t")
         g1 = [keep.tile([P, T], F32, name=f"g1_{r}") for r in range(2)]
+        nc.scalar.dma_start(g1[1][:], gate1[1])
+        pos1_t = load_list(pos1, "pos1_t")
         nc.sync.dma_start(g1[0][:], gate1[0])
         pos2_t = load_list(pos2, "pos2_t")
-        nc.sync.dma_start(g1[1][:], gate1[1])
         offs2_t = load_list(offs2, "offs2_t")
         pos3_t = load_list(pos3, "pos3_t")
         pos4_t = load_list(pos4, "pos4_t")
         g2 = [keep.tile([P, T], F32, name=f"g2_{r}") for r in range(2)]
-        nc.sync.dma_start(g2[0][:], gate2[0])
-        nc.sync.dma_start(g2[1][:], gate2[1])
+        for r in range(2):
+            nc.sync.dma_start(g2[r][:], gate2[r])
 
-        gw = [keep.tile([P, 2 * C], U32, name=f"gw{g}", align_bytes=64) for g in range(3)]
-        gs = [keep.tile([P, 2 * C], U8, name=f"gs{g}", align_bytes=64) for g in range(3)]
-        wp = [keep.tile([P, 2, PACK, P], I32, name=f"wp{g}", align_bytes=64) for g in range(2)]
-        wp_first = keep.tile([P, 2, P], I32, name="wp_first", align_bytes=64)
-        wp_rest = keep.tile([P, 2, PACK - 1, P], I32, name="wp_rest", align_bytes=64)
-        sp = [keep.tile([P, PACK, P], U8, name=f"sp{b}", align_bytes=64) for b in range(2)]
+        gw = [keep.tile([P, 2 * C], U32, name=f"gw{g}", align_bytes=64) for g in range(2)]
+        gw.append(shared.tile([P, 2 * C], U32, name="gw2", align_bytes=64, offset=RAW + 4 * C))
+        gs = [keep.tile([P, 2 * C], U8, name="gs0", align_bytes=64)]
+        gs += [shared.tile([P, 2 * C], U8, name=f"gs{g}", align_bytes=64, offset=RAW * g) for g in (1, 2)]
+        wp = [keep.tile([P, 2, PACK, P], I32, name=f"wp{g}", align_bytes=64) for g in range(3)]
+        sp = keep.tile([P, PACK, P], U8, name="sp", align_bytes=64)
+        sp_first = shared.tile([P, P], U8, name="sp_first", align_bytes=64, offset=RAW + 2 * C)
+        sp_rest = shared.tile([P, PACK - 1, P], U8, name="sp_rest", align_bytes=64, offset=2 * RAW + 2 * C)
 
         def gather_words(g):
             a = 2 * C * g
@@ -117,17 +126,17 @@ def tile_moe_uni_none_kernel(
                 w_raw[g][:].rearrange("p e (m t) -> p e m t", t=PACK),
             )
 
-        def permute_scales(b):
-            nc.vector.tensor_copy(sp[b][:], ws[b][:].bitcast(U8).rearrange("p (m t) -> p t m", t=PACK))
+        def scale_columns(b):
+            return ws[b][:].bitcast(U8).rearrange("p (m t) -> p t m", t=PACK)
 
         def weight(e, t):
             if e < 4:
-                codes = wp[e // 2][:, e % 2, t, :]
+                plane = sp[:, t, :]
             elif t == 0:
-                codes = wp_first[:, e % 2, :]
+                plane = sp_first[:]
             else:
-                codes = wp_rest[:, e % 2, t - 1, :]
-            return codes.bitcast(FP8X4), sp[e // 4][4 * (e % 4) :, t, :]
+                plane = sp_rest[:, t - 1, :]
+            return wp[e // 2][:, e % 2, t, :].bitcast(FP8X4), plane[4 * (e % 4) :, :]
 
         def product(dst, t, bank, a, b, codes, scales):
             col = 0
@@ -161,27 +170,25 @@ def tile_moe_uni_none_kernel(
         gather_words(0)
         gather_words(1)
         permute_words(0)
-        permute_scales(0)
+        nc.vector.tensor_copy(sp[:], scale_columns(0))
         gather_bytes(0, 0, 512)
         product(y, 0, 0, 0, 512, x_codes, x_scale)
-        gather_words(2)
         permute_words(1)
         gather_bytes(1, 0, 512)
         product(y, 0, 4, 512, 1024, x_codes, x_scale)
-        w_last = w_raw[2][:].rearrange("p e (m t) -> p e m t", t=PACK)
-        nc.vector.tensor_copy(wp_first[:], w_last[:, :, :, 0])
-        permute_scales(1)
+        gather_words(2)
+        permute_words(2)
+        nc.vector.tensor_copy(sp_first[:], scale_columns(1)[:, 0, :])
         gather_bytes(2, 0, 256)
         product(y, 0, 5, 1024, 1280, x_codes, x_scale)
         gather_bytes(2, 256, 384)
         product(y, 0, 6, 1280, 1408, x_codes, x_scale)
         gather_bytes(2, 384, 512)
         product(y, 0, 7, 1408, 1536, x_codes, x_scale)
-        nc.vector.tensor_copy(wp_rest[:].rearrange("p e t m -> p e m t"), w_last[:, :, :, 1:PACK])
-        for t in range(1, PACK):
-            product(y, t, t, 0, 512, x_codes, x_scale)
-            product(y, t, 6, 512, 1024, x_codes, x_scale)
-            product(y, t, 7, 1024, 1536, x_codes, x_scale)
+        nc.vector.tensor_copy(sp_rest[:], scale_columns(1)[:, 1:PACK, :])
+        for t, trio in ((1, (1, 0, 4)), (2, (2, 6, 1)), (3, (3, 7, 2))):
+            for g in range(3):
+                product(y, t, trio[g], 512 * g, 512 * (g + 1), x_codes, x_scale)
 
         def weighted(dst, src, pos, gate, a, b):
             nc.vector.tensor_tensor(dst[:, a:b], src[:].indirect(entries(pos, a, b)), gate[:, a:b], MULT)
@@ -218,18 +225,14 @@ def tile_moe_uni_none_kernel(
         for t in range(PACK):
             pa = work.tile([P, T], F32, name="pa")
             pb = work.tile([P, T], F32, name="pb")
-            weighted(pa, y[t], pos1_t, g1[0], 0, 128)
-            weighted(pa, y[t], pos1_t, g1[0], 128, T)
+            weighted(pa, y[t], pos1_t, g1[0], 0, T)
+            for a in (0, HALF):
+                weighted(pb, y[t], pos2_t, g1[1], a, a + HALF)
+            for a in (0, HALF):
+                nc.vector.tensor_tensor(c[t][:, a : a + HALF], pa[:, a : a + HALF], pb[:, a : a + HALF], ADD)
             if t < PACK - 1:
-                weighted(pb, y[t], pos2_t, g1[1], 0, T)
-                nc.vector.tensor_tensor(c[t][:], pa[:], pb[:], ADD)
                 for e in range(E):
                     gather_plane(t, e, 0, C)
-            else:
-                weighted(pb, y[t], pos2_t, g1[1], 0, 640)
-                weighted(pb, y[t], pos2_t, g1[1], 640, T)
-                nc.vector.tensor_tensor(c[t][:, 0:512], pa[:, 0:512], pb[:, 0:512], ADD)
-                nc.vector.tensor_tensor(c[t][:, 512:T], pa[:, 512:T], pb[:, 512:T], ADD)
 
         pieces = [(e, 0, C) for e in range(E - 1)] + [(E - 1, 0, 128), (E - 1, 128, C)]
         for e, a, b in pieces:
@@ -241,9 +244,9 @@ def tile_moe_uni_none_kernel(
         product(z, 0, 2, 1024, 1280, c_codes, c_scale)
         product(z, 0, 3, 1280, 1408, c_codes, c_scale)
         product(z, 0, 4, 1408, 1536, c_codes, c_scale)
-        for t in range(1, PACK):
+        for t, trio in ((1, (3, 4, 5)), (2, (3, 4, 2)), (3, (3, 4, 5))):
             for g in range(3):
-                product(z, t, 3 + g, 512 * g, 512 * (g + 1), c_codes, c_scale)
+                product(z, t, trio[g], 512 * g, 512 * (g + 1), c_codes, c_scale)
 
         out_rows = out.rearrange("(p t) n -> t p n", t=PACK)
         for t in range(PACK):
@@ -266,12 +269,10 @@ def tile_moe_uni_none_kernel(
                     nc.scalar.copy(res[:, a:b], banks[6 + h][:, 0:HALF])
                     nc.sync.dma_start(out_rows[t][:, a:b], res[:, a:b])
             else:
-                weighted(pa, z[t], pos3_t, g2[0], 0, 128)
-                weighted(pa, z[t], pos3_t, g2[0], 128, 512)
-                weighted(pb, z[t], pos4_t, g2[1], 0, 512)
-                weighted(pa, z[t], pos3_t, g2[0], 512, T)
-                nc.vector.tensor_tensor(res[:, 0:512], pa[:, 0:512], pb[:, 0:512], ADD)
-                nc.sync.dma_start(out_rows[t][:, 0:512], res[:, 0:512])
-                weighted(pb, z[t], pos4_t, g2[1], 512, T)
-                nc.vector.tensor_tensor(res[:, 512:T], pa[:, 512:T], pb[:, 512:T], ADD)
-                nc.sync.dma_start(out_rows[t][:, 512:T], res[:, 512:T])
+                weighted(pa, z[t], pos3_t, g2[0], *TAIL[0])
+                for i, (a, b) in enumerate(TAIL):
+                    weighted(pb, z[t], pos4_t, g2[1], a, b)
+                    if i + 1 < len(TAIL):
+                        weighted(pa, z[t], pos3_t, g2[0], *TAIL[i + 1])
+                    nc.vector.tensor_tensor(res[:, a:b], pa[:, a:b], pb[:, a:b], ADD)
+                    nc.sync.dma_start(out_rows[t][:, a:b], res[:, a:b])

@@ -37,7 +37,7 @@ def tile_moe_uni_none_kernel(
     with ExitStack() as ctx:
         lists = ctx.enter_context(tc.tile_pool(name="lists", bufs=1))
         keep = ctx.enter_context(tc.tile_pool(name="keep", bufs=1))
-        work = ctx.enter_context(tc.tile_pool(name="work", bufs=2))
+        work = ctx.enter_context(tc.tile_pool(name="work", bufs=3))
         shared = ctx.enter_context(tc.tile_pool(name="shared", bufs=1))
         psum = ctx.enter_context(tc.psum_pool(name="psum", bufs=1))
 
@@ -81,12 +81,11 @@ def tile_moe_uni_none_kernel(
         ident = keep.tile([P, P], F32, name="ident")
         make_identity(nc, ident[:])
 
-        load_words(0)
         load_scales(0)
         for q in range(4):
             load_token_scales(q, nc.sync if q < 2 else nc.scalar)
-        load_words(1)
-        load_words(2)
+        for g in range(3):
+            load_words(g)
         load_scales(1)
 
         g1 = [keep.tile([P, T], F32, name=f"g1_{r}") for r in range(2)]
@@ -104,11 +103,14 @@ def tile_moe_uni_none_kernel(
         gw = [keep.tile([P, 2 * C], U32, name=f"gw{g}", align_bytes=64) for g in range(2)]
         gw.append(shared.tile([P, 2 * C], U32, name="gw2", align_bytes=64, offset=RAW + 4 * C))
         gs = [keep.tile([P, 2 * C], U8, name="gs0", align_bytes=64)]
-        gs += [shared.tile([P, 2 * C], U8, name=f"gs{g}", align_bytes=64, offset=RAW * g) for g in (1, 2)]
-        wp = [keep.tile([P, 2, PACK, P], I32, name=f"wp{g}", align_bytes=64) for g in range(3)]
+        gs.append(shared.tile([P, 2 * C], U8, name="gs1", align_bytes=64, offset=RAW))
+        gs.append(shared.tile([P, 2 * C], U8, name="gs2", align_bytes=64, offset=RAW + 12 * C))
+        wp = [keep.tile([P, 2, PACK, P], I32, name=f"wp{g}", align_bytes=64) for g in range(2)]
+        wp_first = keep.tile([P, 2, P], I32, name="wp_first", align_bytes=64)
+        wp_rest = keep.tile([P, 2, PACK - 1, P], I32, name="wp_rest", align_bytes=64)
         sp = keep.tile([P, PACK, P], U8, name="sp", align_bytes=64)
         sp_first = shared.tile([P, P], U8, name="sp_first", align_bytes=64, offset=RAW + 2 * C)
-        sp_rest = shared.tile([P, PACK - 1, P], U8, name="sp_rest", align_bytes=64, offset=2 * RAW + 2 * C)
+        sp_rest = keep.tile([P, PACK - 1, P], U8, name="sp_rest", align_bytes=64)
 
         def gather_words(g):
             a = 2 * C * g
@@ -131,12 +133,12 @@ def tile_moe_uni_none_kernel(
 
         def weight(e, t):
             if e < 4:
-                plane = sp[:, t, :]
+                codes, plane = wp[e // 2][:, e % 2, t, :], sp[:, t, :]
             elif t == 0:
-                plane = sp_first[:]
+                codes, plane = wp_first[:, e % 2, :], sp_first[:]
             else:
-                plane = sp_rest[:, t - 1, :]
-            return wp[e // 2][:, e % 2, t, :].bitcast(FP8X4), plane[4 * (e % 4) :, :]
+                codes, plane = wp_rest[:, e % 2, t - 1, :], sp_rest[:, t - 1, :]
+            return codes.bitcast(FP8X4), plane[4 * (e % 4) :, :]
 
         def product(dst, t, bank, a, b, codes, scales):
             col = 0
@@ -177,7 +179,8 @@ def tile_moe_uni_none_kernel(
         gather_bytes(1, 0, 512)
         product(y, 0, 4, 512, 1024, x_codes, x_scale)
         gather_words(2)
-        permute_words(2)
+        w_last = w_raw[2][:].rearrange("p e (m t) -> p e m t", t=PACK)
+        nc.vector.tensor_copy(wp_first[:], w_last[:, :, :, 0])
         nc.vector.tensor_copy(sp_first[:], scale_columns(1)[:, 0, :])
         gather_bytes(2, 0, 256)
         product(y, 0, 5, 1024, 1280, x_codes, x_scale)
@@ -185,6 +188,7 @@ def tile_moe_uni_none_kernel(
         product(y, 0, 6, 1280, 1408, x_codes, x_scale)
         gather_bytes(2, 384, 512)
         product(y, 0, 7, 1408, 1536, x_codes, x_scale)
+        nc.vector.tensor_copy(wp_rest[:].rearrange("p e t m -> p e m t"), w_last[:, :, :, 1:PACK])
         nc.vector.tensor_copy(sp_rest[:], scale_columns(1)[:, 1:PACK, :])
         for t, trio in ((1, (1, 0, 4)), (2, (2, 6, 1)), (3, (3, 7, 2))):
             for g in range(3):
@@ -244,9 +248,12 @@ def tile_moe_uni_none_kernel(
         product(z, 0, 2, 1024, 1280, c_codes, c_scale)
         product(z, 0, 3, 1280, 1408, c_codes, c_scale)
         product(z, 0, 4, 1408, 1536, c_codes, c_scale)
-        for t, trio in ((1, (3, 4, 5)), (2, (3, 4, 2)), (3, (3, 4, 5))):
+        def second_products(t, trio):
             for g in range(3):
                 product(z, t, trio[g], 512 * g, 512 * (g + 1), c_codes, c_scale)
+
+        second_products(1, (3, 4, 5))
+        second_products(2, (3, 4, 2))
 
         out_rows = out.rearrange("(p t) n -> t p n", t=PACK)
         for t in range(PACK):
@@ -268,6 +275,8 @@ def tile_moe_uni_none_kernel(
                         nc.tensor.transpose(banks[6 + h][:, j - a : j - a + P], turned[:, j : j + P], ident[:])
                     nc.scalar.copy(res[:, a:b], banks[6 + h][:, 0:HALF])
                     nc.sync.dma_start(out_rows[t][:, a:b], res[:, a:b])
+                if t == 0:
+                    second_products(3, (3, 4, 5))
             else:
                 weighted(pa, z[t], pos3_t, g2[0], *TAIL[0])
                 for i, (a, b) in enumerate(TAIL):

@@ -23,6 +23,7 @@ PACK = 4
 BANK = 512
 HALF = T // 2
 RAW = 2 * K * 4
+RAW_AT = (0, 2 * RAW, RAW)
 TAIL = ((0, 384), (384, 640), (640, T))
 
 
@@ -53,10 +54,14 @@ def tile_moe_uni_none_kernel(
         nc.vector.memset(ws[0][:], 0)
         nc.vector.memset(ws[1][:], 0)
 
-        offs_t = load_list(offs, "offs_t")
+        xs_rows = x_scales[0].bitcast(I32)
         xw = keep.tile([P, T], I32, name="xw", align_bytes=64)
-        nc.sync.dma_start(xw[:], x_words[0].rearrange("p t d -> p (t d)").bitcast(I32))
-        w_raw = [shared.tile([P, 2, K], I32, name=f"w_raw{g}", align_bytes=64, offset=RAW * g) for g in range(3)]
+        w_raw = [shared.tile([P, 2, K], I32, name=f"w_raw{g}", align_bytes=64, offset=RAW_AT[g]) for g in range(3)]
+
+        def load_token_scales(q, queue):
+            queue.dma_start(
+                xs[32 * q : 32 * q + 32, :], xs_rows[4 * q : 4 * q + 4, :].unsqueeze(0).to_broadcast([8, 4, T // 4])
+            )
 
         def load_words(g):
             nc.sync.dma_start(
@@ -71,22 +76,17 @@ def tile_moe_uni_none_kernel(
                     w_scales[4 * b : 4 * b + n, 0, 4 * q : 4 * q + 4, :].bitcast(I32),
                 )
 
-        xs_rows = x_scales[0].bitcast(I32)
-
-        def load_token_scales(q, queue):
-            queue.dma_start(
-                xs[32 * q : 32 * q + 32, :], xs_rows[4 * q : 4 * q + 4, :].unsqueeze(0).to_broadcast([8, 4, T // 4])
-            )
+        offs_t = load_list(offs, "offs_t")
+        for q in range(4):
+            load_token_scales(q, nc.sync if q < 2 else nc.scalar)
+        nc.sync.dma_start(xw[:], x_words[0].rearrange("p t d -> p (t d)").bitcast(I32))
+        load_scales(0)
+        for g in (0, 2, 1):
+            load_words(g)
+        load_scales(1)
 
         ident = keep.tile([P, P], F32, name="ident")
         make_identity(nc, ident[:])
-
-        load_scales(0)
-        for q in range(4):
-            load_token_scales(q, nc.sync if q < 2 else nc.scalar)
-        for g in range(3):
-            load_words(g)
-        load_scales(1)
 
         g1 = [keep.tile([P, T], F32, name=f"g1_{r}") for r in range(2)]
         nc.scalar.dma_start(g1[1][:], gate1[1])
@@ -100,27 +100,25 @@ def tile_moe_uni_none_kernel(
         for r in range(2):
             nc.sync.dma_start(g2[r][:], gate2[r])
 
+        late = RAW_AT[1]
         gw = [keep.tile([P, 2 * C], U32, name=f"gw{g}", align_bytes=64) for g in range(2)]
-        gw.append(shared.tile([P, 2 * C], U32, name="gw2", align_bytes=64, offset=RAW + 4 * C))
-        gs = [keep.tile([P, 2 * C], U8, name="gs0", align_bytes=64)]
-        gs.append(shared.tile([P, 2 * C], U8, name="gs1", align_bytes=64, offset=RAW))
-        gs.append(shared.tile([P, 2 * C], U8, name="gs2", align_bytes=64, offset=RAW + 12 * C))
+        gw.append(shared.tile([P, 2 * C], U32, name="gw2", align_bytes=64, offset=late + 31 * P))
+        gs = [keep.tile([P, 2 * C], U8, name=f"gs{g}", align_bytes=64) for g in range(2)]
+        gs.append(shared.tile([P, 2 * C], U8, name="gs2", align_bytes=64, offset=late + 27 * P))
         wp = [keep.tile([P, 2, PACK, P], I32, name=f"wp{g}", align_bytes=64) for g in range(2)]
         wp_first = keep.tile([P, 2, P], I32, name="wp_first", align_bytes=64)
-        wp_rest = keep.tile([P, 2, PACK - 1, P], I32, name="wp_rest", align_bytes=64)
+        wp_rest = shared.tile([P, 2, PACK - 1, P], I32, name="wp_rest", align_bytes=64, offset=late)
         sp = keep.tile([P, PACK, P], U8, name="sp", align_bytes=64)
-        sp_first = shared.tile([P, P], U8, name="sp_first", align_bytes=64, offset=RAW + 2 * C)
-        sp_rest = keep.tile([P, PACK - 1, P], U8, name="sp_rest", align_bytes=64)
+        sp_first = keep.tile([P, P], U8, name="sp_first", align_bytes=64)
+        sp_rest = shared.tile([P, PACK - 1, P], U8, name="sp_rest", align_bytes=64, offset=late + 24 * P)
 
-        def gather_words(g):
-            a = 2 * C * g
-            nc.vector.tensor_copy(gw[g][:], xw[:].bitcast(U32).indirect(entries(offs_t, a, a + 2 * C)))
-
-        def gather_bytes(g, a, b):
+        def gather_words(g, a, b):
             base = 2 * C * g
-            nc.vector.tensor_copy(
-                gs[g][:, a:b], xs[:].bitcast(U8).indirect(entries(offs_t, base + a, base + b))
-            )
+            nc.vector.tensor_copy(gw[g][:, a:b], xw[:].bitcast(U32).indirect(entries(offs_t, base + a, base + b)))
+
+        def gather_bytes(g):
+            a = 2 * C * g
+            nc.vector.tensor_copy(gs[g][:], xs[:].bitcast(U8).indirect(entries(offs_t, a, a + 2 * C)))
 
         def permute_words(g):
             nc.vector.tensor_copy(
@@ -140,7 +138,7 @@ def tile_moe_uni_none_kernel(
                 codes, plane = wp_rest[:, e % 2, t - 1, :], sp_rest[:, t - 1, :]
             return codes.bitcast(FP8X4), plane[4 * (e % 4) :, :]
 
-        def product(dst, t, bank, a, b, codes, scales):
+        def product(dst, t, bank, a, b, codes, scales, copy=nc.scalar.copy):
             col = 0
             s = a
             while s < b:
@@ -159,7 +157,7 @@ def tile_moe_uni_none_kernel(
                 )
                 col += n
                 s += n
-            nc.scalar.copy(dst[t][:, a:b], banks[bank][:, 0 : b - a])
+            copy(dst[t][:, a:b], banks[bank][:, 0 : b - a])
 
         y = [keep.tile([P, S], F32, name=f"y{t}") for t in range(PACK)]
 
@@ -169,24 +167,24 @@ def tile_moe_uni_none_kernel(
         def x_scale(a, b):
             return gs[a // (2 * C)][:, a % (2 * C) : a % (2 * C) + b - a]
 
-        gather_words(0)
-        gather_words(1)
-        permute_words(0)
+        gather_bytes(0)
+        gather_bytes(1)
+        gather_words(0, 0, 512)
+        gather_words(1, 0, 512)
         nc.vector.tensor_copy(sp[:], scale_columns(0))
-        gather_bytes(0, 0, 512)
+        permute_words(0)
         product(y, 0, 0, 0, 512, x_codes, x_scale)
-        permute_words(1)
-        gather_bytes(1, 0, 512)
-        product(y, 0, 4, 512, 1024, x_codes, x_scale)
-        gather_words(2)
         w_last = w_raw[2][:].rearrange("p e (m t) -> p e m t", t=PACK)
         nc.vector.tensor_copy(wp_first[:], w_last[:, :, :, 0])
         nc.vector.tensor_copy(sp_first[:], scale_columns(1)[:, 0, :])
-        gather_bytes(2, 0, 256)
+        permute_words(1)
+        product(y, 0, 4, 512, 1024, x_codes, x_scale)
+        gather_bytes(2)
+        gather_words(2, 0, 256)
         product(y, 0, 5, 1024, 1280, x_codes, x_scale)
-        gather_bytes(2, 256, 384)
+        gather_words(2, 256, 384)
         product(y, 0, 6, 1280, 1408, x_codes, x_scale)
-        gather_bytes(2, 384, 512)
+        gather_words(2, 384, 512)
         product(y, 0, 7, 1408, 1536, x_codes, x_scale)
         nc.vector.tensor_copy(wp_rest[:].rearrange("p e t m -> p e m t"), w_last[:, :, :, 1:PACK])
         nc.vector.tensor_copy(sp_rest[:], scale_columns(1)[:, 1:PACK, :])
@@ -229,14 +227,21 @@ def tile_moe_uni_none_kernel(
         for t in range(PACK):
             pa = work.tile([P, T], F32, name="pa")
             pb = work.tile([P, T], F32, name="pb")
-            weighted(pa, y[t], pos1_t, g1[0], 0, T)
-            for a in (0, HALF):
-                weighted(pb, y[t], pos2_t, g1[1], a, a + HALF)
-            for a in (0, HALF):
-                nc.vector.tensor_tensor(c[t][:, a : a + HALF], pa[:, a : a + HALF], pb[:, a : a + HALF], ADD)
             if t < PACK - 1:
+                weighted(pa, y[t], pos1_t, g1[0], 0, T)
+                for a in (0, HALF):
+                    weighted(pb, y[t], pos2_t, g1[1], a, a + HALF)
+                for a in (0, HALF):
+                    nc.vector.tensor_tensor(c[t][:, a : a + HALF], pa[:, a : a + HALF], pb[:, a : a + HALF], ADD)
                 for e in range(E):
                     gather_plane(t, e, 0, C)
+            else:
+                weighted(pa, y[t], pos1_t, g1[0], *TAIL[0])
+                for i, (a, b) in enumerate(TAIL):
+                    weighted(pb, y[t], pos2_t, g1[1], a, b)
+                    if i + 1 < len(TAIL):
+                        weighted(pa, y[t], pos1_t, g1[0], *TAIL[i + 1])
+                    nc.vector.tensor_tensor(c[t][:, a:b], pa[:, a:b], pb[:, a:b], ADD)
 
         pieces = [(e, 0, C) for e in range(E - 1)] + [(E - 1, 0, 128), (E - 1, 128, C)]
         for e, a, b in pieces:
@@ -246,8 +251,8 @@ def tile_moe_uni_none_kernel(
         product(z, 0, 0, 0, 512, c_codes, c_scale)
         product(z, 0, 1, 512, 1024, c_codes, c_scale)
         product(z, 0, 2, 1024, 1280, c_codes, c_scale)
-        product(z, 0, 3, 1280, 1408, c_codes, c_scale)
-        product(z, 0, 4, 1408, 1536, c_codes, c_scale)
+        product(z, 0, 3, 1280, 1408, c_codes, c_scale, nc.vector.tensor_copy)
+        product(z, 0, 4, 1408, 1536, c_codes, c_scale, nc.vector.tensor_copy)
         def second_products(t, trio):
             for g in range(3):
                 product(z, t, trio[g], 512 * g, 512 * (g + 1), c_codes, c_scale)

from contextlib import ExitStack

import concourse.mybir as mybir
from concourse.masks import make_identity

K, T, E, C = 512, 768, 6, 256
S = E * C
FLOPS = 2 * 2 * K * K * S

F32 = mybir.dt.float32
BF16 = mybir.dt.bfloat16
I32 = mybir.dt.int32
U32 = mybir.dt.uint32
U16 = mybir.dt.uint16
U8 = mybir.dt.uint8
FP8X4 = mybir.dt.float8_e4m3fn_x4
MULT = mybir.AluOpType.mult
ADD = mybir.AluOpType.add
COPY = mybir.ActivationFunctionType.Copy

P = 128
PACK = 4
BANK = 512
HALF = T // 2
RAW = 2 * K * 4
RAW_AT = (0, 2 * RAW, RAW)
TAIL = ((0, 384), (384, 640), (640, T))


def entries(tile, a, b):
    return tile[:, a // 16 : b // 16]


def tile_moe_uni_none_kernel(
    tc, x_words, x_scales, w_words, w_scales, gate1, gate2, offs, pos1, pos2, offs2, pos3, pos4, out
):
    nc = tc.nc
    with ExitStack() as ctx:
        lists = ctx.enter_context(tc.tile_pool(name="lists", bufs=1))
        keep = ctx.enter_context(tc.tile_pool(name="keep", bufs=1))
        work = ctx.enter_context(tc.tile_pool(name="work", bufs=3))
        shared = ctx.enter_context(tc.tile_pool(name="shared", bufs=1))
        psum = ctx.enter_context(tc.psum_pool(name="psum", bufs=1))

        banks = [psum.tile([P, BANK], F32, name=f"bank{b}") for b in range(8)]

        def load_list(src, name):
            tile = lists.tile([P, src.shape[1]], U16, name=name)
            nc.sync.dma_start(tile[:], src)
            return tile

        xs = keep.tile([P, T // 4], I32, name="xs", align_bytes=64)
        ws = [keep.tile([P, K // 4], I32, name=f"ws{b}", align_bytes=64) for b in range(2)]
        nc.vector.memset(ws[0][:], 0)
        nc.vector.memset(ws[1][:], 0)

        xs_rows = x_scales[0].bitcast(I32)
        xw = keep.tile([P, T], I32, name="xw", align_bytes=64)
        w_raw = [shared.tile([P, 2, K], I32, name=f"w_raw{g}", align_bytes=64, offset=RAW_AT[g]) for g in range(3)]

        def load_token_scales(q, queue):
            queue.dma_start(
                xs[32 * q : 32 * q + 32, :], xs_rows[4 * q : 4 * q + 4, :].unsqueeze(0).to_broadcast([8, 4, T // 4])
            )

        def load_words(g):
            nc.sync.dma_start(
                w_raw[g][:], w_words[2 * g : 2 * g + 2, 0].rearrange("e p i d -> p e (i d)").bitcast(I32)
            )

        def load_scales(b):
            n = min(4, E - 4 * b)
            for q in range(4):
                nc.scalar.dma_start(
                    ws[b][32 * q : 32 * q + 4 * n, :],
                    w_scales[4 * b : 4 * b + n, 0, 4 * q : 4 * q + 4, :].bitcast(I32),
                )

        offs_t = load_list(offs, "offs_t")
        for q in range(4):
            load_token_scales(q, nc.sync if q < 2 else nc.scalar)
        nc.sync.dma_start(xw[:], x_words[0].rearrange("p t d -> p (t d)").bitcast(I32))
        load_scales(0)
        for g in (0, 2, 1):
            load_words(g)
        load_scales(1)

        ident = keep.tile([P, P], F32, name="ident")
        make_identity(nc, ident[:])

        g1 = [keep.tile([P, T], F32, name=f"g1_{r}") for r in range(2)]
        nc.scalar.dma_start(g1[1][:], gate1[1])
        pos1_t = load_list(pos1, "pos1_t")
        nc.sync.dma_start(g1[0][:], gate1[0])
        pos2_t = load_list(pos2, "pos2_t")
        offs2_t = load_list(offs2, "offs2_t")
        pos3_t = load_list(pos3, "pos3_t")
        pos4_t = load_list(pos4, "pos4_t")
        g2 = [keep.tile([P, T], F32, name=f"g2_{r}") for r in range(2)]
        for r in range(2):
            nc.sync.dma_start(g2[r][:], gate2[r])

        late = RAW_AT[1]
        gw = [keep.tile([P, 2 * C], U32, name=f"gw{g}", align_bytes=64) for g in range(2)]
        gw.append(shared.tile([P, 2 * C], U32, name="gw2", align_bytes=64, offset=late + 31 * P))
        gs = [keep.tile([P, 2 * C], U8, name=f"gs{g}", align_bytes=64) for g in range(2)]
        gs.append(shared.tile([P, 2 * C], U8, name="gs2", align_bytes=64, offset=late + 27 * P))
        wp = [keep.tile([P, 2, PACK, P], I32, name=f"wp{g}", align_bytes=64) for g in range(2)]
        wp_first = keep.tile([P, 2, P], I32, name="wp_first", align_bytes=64)
        wp_rest = shared.tile([P, 2, PACK - 1, P], I32, name="wp_rest", align_bytes=64, offset=late)
        sp = keep.tile([P, PACK, P], U8, name="sp", align_bytes=64)
        sp_first = keep.tile([P, P], U8, name="sp_first", align_bytes=64)
        sp_rest = shared.tile([P, PACK - 1, P], U8, name="sp_rest", align_bytes=64, offset=late + 24 * P)

        def gather_words(g, a, b):
            base = 2 * C * g
            nc.vector.tensor_copy(gw[g][:, a:b], xw[:].bitcast(U32).indirect(entries(offs_t, base + a, base + b)))

        def gather_bytes(g):
            a = 2 * C * g
            nc.vector.tensor_copy(gs[g][:], xs[:].bitcast(U8).indirect(entries(offs_t, a, a + 2 * C)))

        def permute_words(g):
            nc.vector.tensor_copy(
                wp[g][:].rearrange("p e t m -> p e m t"),
                w_raw[g][:].rearrange("p e (m t) -> p e m t", t=PACK),
            )

        def scale_columns(b):
            return ws[b][:].bitcast(U8).rearrange("p (m t) -> p t m", t=PACK)

        def weight(e, t):
            if e < 4:
                codes, plane = wp[e // 2][:, e % 2, t, :], sp[:, t, :]
            elif t == 0:
                codes, plane = wp_first[:, e % 2, :], sp_first[:]
            else:
                codes, plane = wp_rest[:, e % 2, t - 1, :], sp_rest[:, t - 1, :]
            return codes.bitcast(FP8X4), plane[4 * (e % 4) :, :]

        def product(dst, t, bank, a, b, codes, scales, copy=nc.scalar.copy):
            col = 0
            s = a
            while s < b:
                e = s // C
                n = min(b, (e + 1) * C) - s
                lhs, lhs_scale = weight(e, t)
                rhs, rhs_scale = codes(s, s + n), scales(s, s + n)
                nc.tensor.matmul_mx(
                    out=banks[bank][:, col : col + n],
                    lhsT=lhs,
                    lhsT_scale=lhs_scale,
                    rhs=rhs.bitcast(FP8X4),
                    rhs_scale=rhs_scale,
                    start=True,
                    stop=True,
                )
                col += n
                s += n
            copy(dst[t][:, a:b], banks[bank][:, 0 : b - a])

        y = [keep.tile([P, S], F32, name=f"y{t}") for t in range(PACK)]

        def x_codes(a, b):
            return gw[a // (2 * C)][:, a % (2 * C) : a % (2 * C) + b - a]

        def x_scale(a, b):
            return gs[a // (2 * C)][:, a % (2 * C) : a % (2 * C) + b - a]

        gather_bytes(0)
        gather_bytes(1)
        gather_words(0, 0, 512)
        gather_words(1, 0, 512)
        nc.vector.tensor_copy(sp[:], scale_columns(0))
        permute_words(0)
        product(y, 0, 0, 0, 512, x_codes, x_scale)
        w_last = w_raw[2][:].rearrange("p e (m t) -> p e m t", t=PACK)
        nc.vector.tensor_copy(wp_first[:], w_last[:, :, :, 0])
        nc.vector.tensor_copy(sp_first[:], scale_columns(1)[:, 0, :])
        permute_words(1)
        product(y, 0, 4, 512, 1024, x_codes, x_scale)
        gather_bytes(2)
        gather_words(2, 0, 256)
        product(y, 0, 5, 1024, 1280, x_codes, x_scale)
        gather_words(2, 256, 384)
        product(y, 0, 6, 1280, 1408, x_codes, x_scale)
        gather_words(2, 384, 512)
        product(y, 0, 7, 1408, 1536, x_codes, x_scale)
        nc.vector.tensor_copy(wp_rest[:].rearrange("p e t m -> p e m t"), w_last[:, :, :, 1:PACK])
        nc.vector.tensor_copy(sp_rest[:], scale_columns(1)[:, 1:PACK, :])
        for t, trio in ((1, (1, 0, 4)), (2, (2, 6, 1)), (3, (3, 7, 2))):
            for g in range(3):
                product(y, t, trio[g], 512 * g, 512 * (g + 1), x_codes, x_scale)

        def weighted(dst, src, pos, gate, a, b):
            nc.vector.tensor_tensor(dst[:, a:b], src[:].indirect(entries(pos, a, b)), gate[:, a:b], MULT)

        c = [keep.tile([P, T], BF16, name=f"c{t}", align_bytes=64) for t in range(PACK)]
        pairs = [keep.tile([P, 2, C, 2], BF16, name=f"pairs{e}", align_bytes=64) for e in range(E)]
        quads = [keep.tile([P, C, PACK], BF16, name=f"quads{e}", align_bytes=64) for e in range(E)]
        cw = [keep.tile([P, C], U32, name=f"cw{e}", align_bytes=64) for e in range(E)]
        cs = [keep.tile([P, C], U8, name=f"cs{e}", align_bytes=64) for e in range(E)]
        z = [keep.tile([P, S], F32, name=f"z{t}") for t in range(PACK)]

        def c_codes(a, b):
            return cw[a // C][:, a % C : a % C + b - a]

        def c_scale(a, b):
            return cs[a // C][:, a % C : a % C + b - a]

        def gather_plane(t, e, a, b):
            nc.scalar.activation(
                pairs[e][:, t // 2, a:b, t % 2], c[t][:].indirect(entries(offs2_t, e * C + a, e * C + b)), COPY
            )

        def quantise(e, a, b):
            nc.vector.tensor_copy(
                quads[e][:, a:b, :].rearrange("p s (u j) -> p s u j", u=2),
                pairs[e][:, :, a:b, :].rearrange("p u s j -> p s u j"),
            )
            nc.vector.quantize_mx(
                out=cw[e][:, a:b].bitcast(FP8X4),
                scales=cs[e][:, a:b],
                in_=quads[e][:, a:b, :].rearrange("p s j -> p (s j)"),
            )

        for t in range(PACK):
            pa = work.tile([P, T], F32, name="pa")
            pb = work.tile([P, T], F32, name="pb")
            if t < PACK - 1:
                weighted(pa, y[t], pos1_t, g1[0], 0, T)
                for a in (0, HALF):
                    weighted(pb, y[t], pos2_t, g1[1], a, a + HALF)
                for a in (0, HALF):
                    nc.vector.tensor_tensor(c[t][:, a : a + HALF], pa[:, a : a + HALF], pb[:, a : a + HALF], ADD)
                for e in range(E):
                    gather_plane(t, e, 0, C)
            else:
                weighted(pa, y[t], pos1_t, g1[0], *TAIL[0])
                for i, (a, b) in enumerate(TAIL):
                    weighted(pb, y[t], pos2_t, g1[1], a, b)
                    if i + 1 < len(TAIL):
                        weighted(pa, y[t], pos1_t, g1[0], *TAIL[i + 1])
                    nc.vector.tensor_tensor(c[t][:, a:b], pa[:, a:b], pb[:, a:b], ADD)

        pieces = [(e, 0, C) for e in range(E - 1)] + [(E - 1, 0, 128), (E - 1, 128, C)]
        for e, a, b in pieces:
            gather_plane(PACK - 1, e, a, b)
        for e, a, b in pieces:
            quantise(e, a, b)
        product(z, 0, 0, 0, 512, c_codes, c_scale)
        product(z, 0, 1, 512, 1024, c_codes, c_scale)
        product(z, 0, 2, 1024, 1280, c_codes, c_scale)
        product(z, 0, 3, 1280, 1408, c_codes, c_scale, nc.vector.tensor_copy)
        product(z, 0, 4, 1408, 1536, c_codes, c_scale, nc.vector.tensor_copy)
        def second_products(t, trio):
            for g in range(3):
                product(z, t, trio[g], 512 * g, 512 * (g + 1), c_codes, c_scale)

        second_products(1, (3, 4, 5))
        second_products(2, (3, 4, 2))

        out_rows = out.rearrange("(p t) n -> t p n", t=PACK)
        for t in range(PACK):
            pa = work.tile([P, T], F32, name="pa")
            pb = work.tile([P, T], F32, name="pb")
            res = keep.tile([P, T], F32, name=f"res{t}")
            if t < PACK - 1:
                turned = work.tile([P, T], F32, name="turned")
                for h in range(2):
                    a, b = h * HALF, (h + 1) * HALF
                    weighted(pa, z[t], pos3_t, g2[0], a, b)
                    weighted(pb, z[t], pos4_t, g2[1], a, b)
                    for j in range(a, b, P):
                        dst = banks[h][:, j - a : j - a + P]
                        nc.tensor.matmul(dst, pa[:, j : j + P], ident[:], start=True, stop=False, is_transpose=True)
                        nc.tensor.matmul(dst, pb[:, j : j + P], ident[:], start=False, stop=True, is_transpose=True)
                    nc.scalar.copy(turned[:, a:b], banks[h][:, 0:HALF])
                    for j in range(a, b, P):
                        nc.tensor.transpose(banks[6 + h][:, j - a : j - a + P], turned[:, j : j + P], ident[:])
                    nc.scalar.copy(res[:, a:b], banks[6 + h][:, 0:HALF])
                    nc.sync.dma_start(out_rows[t][:, a:b], res[:, a:b])
                if t == 0:
                    second_products(3, (3, 4, 5))
            else:
                weighted(pa, z[t], pos3_t, g2[0], *TAIL[0])
                for i, (a, b) in enumerate(TAIL):
                    weighted(pb, z[t], pos4_t, g2[1], a, b)
                    if i + 1 < len(TAIL):
                        weighted(pa, z[t], pos3_t, g2[0], *TAIL[i + 1])
                    nc.vector.tensor_tensor(res[:, a:b], pa[:, a:b], pb[:, a:b], ADD)
                    nc.sync.dma_start(out_rows[t][:, a:b], res[:, a:b])
